import numpy as np
import ml_dtypes

BF16 = ml_dtypes.bfloat16


def bf(x):
    return np.asarray(x, np.float32).astype(BF16)


def f32(x):
    return np.asarray(x, np.float32)


def f64(x):
    return np.asarray(x).astype(np.float64)


def striped(idx):
    return np.tile(idx.reshape(-1, 16).T, (8, 1))


def rows(idx, k):
    return np.tile(idx, (k, 1))


def look(tab, idx):
    return np.take_along_axis(f64(tab), rows(idx, len(tab)), axis=1)


K, S, V, N, M = 128, 2048, 1536, 1536, 128


def silu(v):
    return v / (1.0 + np.exp(-v))


def setup_inputs():
    return {"tab": f32(np.random.standard_normal((2, K, S))), "w": bf(np.random.standard_normal((K, M)) / np.sqrt(K)), "b": f32(0.5 * np.random.standard_normal((M, 1))), "offs": striped(np.random.permutation(S)[:N])}


def reference(tab, w, b, offs):
    idx = offs[:16].T.reshape(-1)
    x = (np.minimum(np.maximum(look(tab[0], idx), -1.25), 1.0)) * (silu(look(tab[1], idx)))
    return np.maximum(f64(w).T @ x + f64(b), 0.0)

@@ -1,0 +1,45 @@
+import concourse.mybir as mybir
+
+F32, BF16, U16 = mybir.dt.float32, mybir.dt.bfloat16, mybir.dt.uint16
+ALU = mybir.AluOpType
+ACT = mybir.ActivationFunctionType
+
+ROWS, PLACES, PICKS, OUT_ROWS = 128, 2048, 1536, 128
+FLOPS = 2 * ROWS * OUT_ROWS * PICKS
+LOW, HIGH = -1.25, 1.0
+PIECE = 512
+PER_COLUMN = 16
+
+
+def tile_lookup_vg_clipsilu_relu_kernel(tc, tab, w, b, offs, out):
+    nc = tc.nc
+    pieces = PICKS // PIECE
+    with (
+        tc.tile_pool(name="held", bufs=1) as held,
+        tc.tile_pool(name="work", bufs=pieces) as work,
+        tc.psum_pool(name="psum", bufs=pieces) as psum,
+    ):
+        offsets = held.tile([ROWS, PICKS // PER_COLUMN], U16)
+        values = held.tile([ROWS, PLACES], F32)
+        gates = held.tile([ROWS, PLACES], F32)
+        weights = held.tile([ROWS, OUT_ROWS], BF16)
+        bias = held.tile([OUT_ROWS, 1], F32)
+        nc.sync.dma_start(offsets[:], offs)
+        nc.sync.dma_start(values[:], tab[0])
+        nc.sync.dma_start(gates[:], tab[1])
+        nc.sync.dma_start(weights[:], w)
+        nc.sync.dma_start(bias[:], b)
+
+        for p in range(pieces):
+            picks = offsets[:, p * PIECE // PER_COLUMN : (p + 1) * PIECE // PER_COLUMN]
+            clamped = work.tile([ROWS, PIECE], F32)
+            nc.vector.tensor_scalar(clamped[:], values[:].indirect(picks), LOW, HIGH, ALU.max, ALU.min)
+            gated = work.tile([ROWS, PIECE], F32)
+            nc.scalar.activation(gated[:], gates[:].indirect(picks), ACT.Silu)
+            x = work.tile([ROWS, PIECE], BF16)
+            nc.vector.tensor_tensor(x[:], clamped[:], gated[:], ALU.mult)
+            product = psum.tile([OUT_ROWS, PIECE], F32)
+            nc.tensor.matmul(product[:], weights[:], x[:], start=True, stop=True)
+            result = work.tile([OUT_ROWS, PIECE], F32)
+            nc.scalar.activation(result[:], product[:], ACT.Relu, bias=bias[:])
+            nc.sync.dma_start(out[:, p * PIECE : (p + 1) * PIECE], result[:])

@@ -30,6 +30,11 @@ def tile_lookup_vg_clipsilu_relu_kernel(tc, tab, w, b, offs, out):
         nc.sync.dma_start(weights[:], w)
         nc.sync.dma_start(bias[:], b)
 
+        warm_in = held.tile([ROWS, 1], F32)
+        warm_out = held.tile([ROWS, 1], F32)
+        nc.vector.memset(warm_in[:], 0.0)
+        nc.scalar.activation(warm_out[:], warm_in[:], ACT.Silu)
+
         for p in range(pieces):
             picks = offsets[:, p * PIECE // PER_COLUMN : (p + 1) * PIECE // PER_COLUMN]
             clamped = work.tile([ROWS, PIECE], F32)

@@ -1,3 +1,5 @@
+import itertools
+
 import concourse.mybir as mybir
 
 F32, BF16, U16 = mybir.dt.float32, mybir.dt.bfloat16, mybir.dt.uint16
@@ -8,6 +10,7 @@ ROWS, PLACES, PICKS, OUT_ROWS = 128, 2048, 1536, 128
 FLOPS = 2 * ROWS * OUT_ROWS * PICKS
 LOW, HIGH = -1.25, 1.0
 PIECE = 512
+STEPS = (128,) * 12
 PER_COLUMN = 16
 
 
@@ -16,16 +19,15 @@ def tile_lookup_vg_clipsilu_relu_kernel(tc, tab, w, b, offs, out):
     pieces = PICKS // PIECE
     with (
         tc.tile_pool(name="held", bufs=1) as held,
-        tc.tile_pool(name="work", bufs=pieces) as work,
-        tc.psum_pool(name="psum", bufs=pieces) as psum,
+        tc.psum_pool(name="psum", bufs=min(len(STEPS), 8)) as psum,
     ):
         offsets = held.tile([ROWS, PICKS // PER_COLUMN], U16)
         values = held.tile([ROWS, PLACES], F32)
         gates = held.tile([ROWS, PLACES], F32)
         weights = held.tile([ROWS, OUT_ROWS], BF16)
         bias = held.tile([OUT_ROWS, 1], F32)
-        nc.sync.dma_start(offsets[:], offs)
         nc.sync.dma_start(values[:], tab[0])
+        nc.sync.dma_start(offsets[:], offs)
         nc.sync.dma_start(gates[:], tab[1])
         nc.sync.dma_start(weights[:], w)
         nc.sync.dma_start(bias[:], b)
@@ -35,16 +37,27 @@ def tile_lookup_vg_clipsilu_relu_kernel(tc, tab, w, b, offs, out):
         nc.vector.memset(warm_in[:], 0.0)
         nc.scalar.activation(warm_out[:], warm_in[:], ACT.Silu)
 
+        clamped = held.tile([ROWS, PICKS], F32)
+        gated = held.tile([ROWS, PICKS], F32)
         for p in range(pieces):
             picks = offsets[:, p * PIECE // PER_COLUMN : (p + 1) * PIECE // PER_COLUMN]
-            clamped = work.tile([ROWS, PIECE], F32)
-            nc.vector.tensor_scalar(clamped[:], values[:].indirect(picks), LOW, HIGH, ALU.max, ALU.min)
-            gated = work.tile([ROWS, PIECE], F32)
-            nc.scalar.activation(gated[:], gates[:].indirect(picks), ACT.Silu)
-            x = work.tile([ROWS, PIECE], BF16)
-            nc.vector.tensor_tensor(x[:], clamped[:], gated[:], ALU.mult)
-            product = psum.tile([OUT_ROWS, PIECE], F32)
-            nc.tensor.matmul(product[:], weights[:], x[:], start=True, stop=True)
-            result = work.tile([OUT_ROWS, PIECE], F32)
-            nc.scalar.activation(result[:], product[:], ACT.Relu, bias=bias[:])
-            nc.sync.dma_start(out[:, p * PIECE : (p + 1) * PIECE], result[:])
+            cols = slice(p * PIECE, (p + 1) * PIECE)
+            nc.vector.tensor_scalar(clamped[:, cols], values[:].indirect(picks), LOW, HIGH, ALU.max, ALU.min)
+            nc.scalar.activation(gated[:, cols], gates[:].indirect(picks), ACT.Silu)
+
+        x = held.tile([ROWS, PICKS], BF16)
+        result = held.tile([OUT_ROWS, PICKS], F32)
+        starts = list(itertools.accumulate(STEPS, initial=0))
+        stored = 0
+        for lo, hi in zip(starts, starts[1:]):
+            cols = slice(lo, hi)
+            nc.vector.tensor_tensor(x[:, cols], clamped[:, cols], gated[:, cols], ALU.mult)
+            product = psum.tile([OUT_ROWS, hi - lo], F32)
+            nc.tensor.matmul(product[:], weights[:], x[:, cols], start=True, stop=True)
+            if hi <= PIECE or hi == PICKS:
+                nc.vector.tensor_scalar(result[:, cols], product[:], bias[:], 0.0, ALU.add, ALU.max)
+            else:
+                nc.scalar.activation(result[:, cols], product[:], ACT.Relu, bias=bias[:])
+            if hi % 256 == 0 or hi > PICKS - 256:
+                nc.sync.dma_start(out[:, stored:hi], result[:, stored:hi])
+                stored = hi

@@ -1,5 +1,3 @@
-import itertools
-
 import concourse.mybir as mybir
 
 F32, BF16, U16 = mybir.dt.float32, mybir.dt.bfloat16, mybir.dt.uint16
@@ -9,17 +7,18 @@ ACT = mybir.ActivationFunctionType
 ROWS, PLACES, PICKS, OUT_ROWS = 128, 2048, 1536, 128
 FLOPS = 2 * ROWS * OUT_ROWS * PICKS
 LOW, HIGH = -1.25, 1.0
-PIECE = 512
-STEPS = (128,) * 12
 PER_COLUMN = 16
+PIECE = 512
+STEP = 128
+STORE = 256
+PSUM_BANKS = 8
 
 
 def tile_lookup_vg_clipsilu_relu_kernel(tc, tab, w, b, offs, out):
     nc = tc.nc
-    pieces = PICKS // PIECE
     with (
         tc.tile_pool(name="held", bufs=1) as held,
-        tc.psum_pool(name="psum", bufs=min(len(STEPS), 8)) as psum,
+        tc.psum_pool(name="psum", bufs=PSUM_BANKS) as psum,
     ):
         offsets = held.tile([ROWS, PICKS // PER_COLUMN], U16)
         values = held.tile([ROWS, PLACES], F32)
@@ -39,25 +38,22 @@ def tile_lookup_vg_clipsilu_relu_kernel(tc, tab, w, b, offs, out):
 
         clamped = held.tile([ROWS, PICKS], F32)
         gated = held.tile([ROWS, PICKS], F32)
-        for p in range(pieces):
-            picks = offsets[:, p * PIECE // PER_COLUMN : (p + 1) * PIECE // PER_COLUMN]
-            cols = slice(p * PIECE, (p + 1) * PIECE)
+        for lo in range(0, PICKS, PIECE):
+            cols = slice(lo, lo + PIECE)
+            picks = offsets[:, lo // PER_COLUMN : (lo + PIECE) // PER_COLUMN]
             nc.vector.tensor_scalar(clamped[:, cols], values[:].indirect(picks), LOW, HIGH, ALU.max, ALU.min)
             nc.scalar.activation(gated[:, cols], gates[:].indirect(picks), ACT.Silu)
 
         x = held.tile([ROWS, PICKS], BF16)
         result = held.tile([OUT_ROWS, PICKS], F32)
-        starts = list(itertools.accumulate(STEPS, initial=0))
-        stored = 0
-        for lo, hi in zip(starts, starts[1:]):
-            cols = slice(lo, hi)
-            nc.vector.tensor_tensor(x[:, cols], clamped[:, cols], gated[:, cols], ALU.mult)
-            product = psum.tile([OUT_ROWS, hi - lo], F32)
-            nc.tensor.matmul(product[:], weights[:], x[:, cols], start=True, stop=True)
+        for lo in range(0, PICKS, STEP):
+            hi = lo + STEP
+            nc.vector.tensor_tensor(x[:, lo:hi], clamped[:, lo:hi], gated[:, lo:hi], ALU.mult)
+            product = psum.tile([OUT_ROWS, STEP], F32)
+            nc.tensor.matmul(product[:], weights[:], x[:, lo:hi], start=True, stop=True)
             if hi <= PIECE or hi == PICKS:
-                nc.vector.tensor_scalar(result[:, cols], product[:], bias[:], 0.0, ALU.add, ALU.max)
+                nc.vector.tensor_scalar(result[:, lo:hi], product[:], bias[:], 0.0, ALU.add, ALU.max)
             else:
-                nc.scalar.activation(result[:, cols], product[:], ACT.Relu, bias=bias[:])
-            if hi % 256 == 0 or hi > PICKS - 256:
-                nc.sync.dma_start(out[:, stored:hi], result[:, stored:hi])
-                stored = hi
+                nc.scalar.activation(result[:, lo:hi], product[:], ACT.Relu, bias=bias[:])
+            if hi % STORE == 0:
+                nc.sync.dma_start(out[:, hi - STORE : hi], result[:, hi - STORE : hi])

import concourse.mybir as mybir

F32, BF16, U16 = mybir.dt.float32, mybir.dt.bfloat16, mybir.dt.uint16
ALU = mybir.AluOpType
ACT = mybir.ActivationFunctionType

ROWS, PLACES, PICKS, OUT_ROWS = 128, 2048, 1536, 128
FLOPS = 2 * ROWS * OUT_ROWS * PICKS
LOW, HIGH = -1.25, 1.0
PER_COLUMN = 16
PIECE = 512
STEP = 128
STORE = 256
PSUM_BANKS = 8


def tile_lookup_vg_clipsilu_relu_kernel(tc, tab, w, b, offs, out):
    nc = tc.nc
    with (
        tc.tile_pool(name="held", bufs=1) as held,
        tc.psum_pool(name="psum", bufs=PSUM_BANKS) as psum,
    ):
        offsets = held.tile([ROWS, PICKS // PER_COLUMN], U16)
        values = held.tile([ROWS, PLACES], F32)
        gates = held.tile([ROWS, PLACES], F32)
        weights = held.tile([ROWS, OUT_ROWS], BF16)
        bias = held.tile([OUT_ROWS, 1], F32)
        nc.sync.dma_start(values[:], tab[0])
        nc.sync.dma_start(offsets[:], offs)
        nc.sync.dma_start(gates[:], tab[1])
        nc.sync.dma_start(weights[:], w)
        nc.sync.dma_start(bias[:], b)

        warm_in = held.tile([ROWS, 1], F32)
        warm_out = held.tile([ROWS, 1], F32)
        nc.vector.memset(warm_in[:], 0.0)
        nc.scalar.activation(warm_out[:], warm_in[:], ACT.Silu)

        clamped = held.tile([ROWS, PICKS], F32)
        gated = held.tile([ROWS, PICKS], F32)
        for lo in range(0, PICKS, PIECE):
            cols = slice(lo, lo + PIECE)
            picks = offsets[:, lo // PER_COLUMN : (lo + PIECE) // PER_COLUMN]
            nc.vector.tensor_scalar(clamped[:, cols], values[:].indirect(picks), LOW, HIGH, ALU.max, ALU.min)
            nc.scalar.activation(gated[:, cols], gates[:].indirect(picks), ACT.Silu)

        x = held.tile([ROWS, PICKS], BF16)
        result = held.tile([OUT_ROWS, PICKS], F32)
        for lo in range(0, PICKS, STEP):
            hi = lo + STEP
            nc.vector.tensor_tensor(x[:, lo:hi], clamped[:, lo:hi], gated[:, lo:hi], ALU.mult)
            product = psum.tile([OUT_ROWS, STEP], F32)
            nc.tensor.matmul(product[:], weights[:], x[:, lo:hi], start=True, stop=True)
            if hi <= PIECE or hi == PICKS:
                nc.vector.tensor_scalar(result[:, lo:hi], product[:], bias[:], 0.0, ALU.add, ALU.max)
            else:
                nc.scalar.activation(result[:, lo:hi], product[:], ACT.Relu, bias=bias[:])
            if hi % STORE == 0:
                nc.sync.dma_start(out[:, hi - STORE : hi], result[:, hi - STORE : hi])
